import numpy as np
import ml_dtypes


def mxq(x, axis, fmt="e4m3"):
    dtype, down = {"e4m3": (ml_dtypes.float8_e4m3fn, 7), "e5m2": (ml_dtypes.float8_e5m2, 14)}[fmt]
    v = np.moveaxis(np.asarray(x, np.float32).astype(ml_dtypes.bfloat16).astype(np.float64), axis, -1)
    blocks = v.reshape(v.shape[:-1] + (-1, 32))
    amax = np.abs(blocks).max(-1, keepdims=True)
    byte = np.maximum(np.where(amax > 0, np.frexp(amax)[1] - 1 + 127, 0) - down, 1)
    scale = np.exp2(byte - 127.0)
    codes = (blocks / scale).astype(np.float32).astype(dtype).astype(np.float64)
    return np.moveaxis((codes * scale).reshape(v.shape), -1, axis)


WIDE = False


def mx_kscale(k):
    if not WIDE:
        return np.ones(k)
    levels = np.array([10, -10, 5, -5, 0])
    if k % 512:
        return np.exp2(np.random.permutation(np.resize(levels, k // 32))).repeat(32)
    a = np.empty((k // 512, 16))
    for p in range(k // 512):
        a[p, :8] = np.random.permutation(np.resize(levels, 8))
        for g in range(8):
            far = levels[np.abs(levels - a[p, g]) >= 10]
            a[p, g + 8] = far[np.random.randint(len(far))]
    return np.exp2(a.ravel()).repeat(32)


def f64(x):
    return np.asarray(x).astype(np.float64)


def striped(idx):
    return np.tile(idx.reshape(-1, 16).T, (8, 1)).astype(np.uint16)


def unstriped(offs):
    return offs[:16].T.reshape(-1).astype(np.int64)


def striped8(idx):
    return np.concatenate([x.reshape(-1, 16).T for x in idx]).astype(np.uint16)


def runs(offs, k):
    lists = np.stack([offs[16 * r : 16 * r + 16].T.reshape(-1) for r in range(8)]).astype(np.int64)
    return lists[np.arange(k) % 512 // 64]


def pack_weight(w):
    k, n = w.shape
    w = f64(np.asarray(w, np.float32).astype(ml_dtypes.bfloat16)).reshape(k // 32, 32, n)
    amax = np.abs(w).max(1)
    byte = np.clip(np.where(amax > 0, np.frexp(amax)[1] - 1 + 127 - 7, 1), 1, 254)
    scaled = (w * np.exp2(127.0 - byte)[:, None, :]).reshape(k, n).astype(np.float32)
    words = np.ascontiguousarray(scaled.reshape(k // 512, 128, 4, n).transpose(0, 1, 3, 2)).astype(ml_dtypes.float8_e4m3fn).view(np.uint8)
    return words, np.ascontiguousarray(byte.astype(np.uint8).reshape(k // 512, 16, n))


def unpack_weight(words, scales):
    g, p, n, _ = words.shape
    vals = np.ascontiguousarray(words).view(ml_dtypes.float8_e4m3fn).astype(np.float64) * np.repeat(np.exp2(scales.astype(np.float64) - 127.0), 8, axis=1)[..., None]
    return vals.transpose(0, 1, 3, 2).reshape(g * 512, n)


def relu(v):
    return np.maximum(v, 0.0)


def sigmoid(v):
    return 1.0 / (1.0 + np.exp(-np.maximum(v, -700.0)))

def planes(y):
    n, m = y.shape
    v = y.astype(np.float32).astype(ml_dtypes.bfloat16).astype(np.float64).reshape(n // 32, 32, m)
    top = np.abs(v).max(1)
    byte = np.clip(np.where(top > 0, np.frexp(top)[1] - 1 + 127 - 7, 1), 1, 254)
    codes = (v * np.exp2(127.0 - byte)[:, None, :]).reshape(n, m).astype(np.float32).astype(ml_dtypes.float8_e4m3fn).view(np.uint8)
    words = codes.reshape(n // 512, 128, 4, m).transpose(0, 1, 3, 2)
    return np.ascontiguousarray(words), np.ascontiguousarray(byte.astype(np.uint8).reshape(n // 512, 16, m))


K, T, S, N, H = 512, 2048, 512, 512, 512


def setup_inputs():
    n = np.random.standard_normal
    s = mx_kscale(K)[:, None]
    u = mx_kscale(H)
    packed_xT = pack_weight(n((K, T)) * s)
    packed_w2 = pack_weight(n((K, H)) / np.sqrt(K) / s)
    packed_w3 = pack_weight(n((H, N)) / np.sqrt(H) / u[:, None])
    return {
        "x_words": packed_xT[0],
        "x_scales": packed_xT[1],
        "w1": (n((K, H)) / np.sqrt(K) / s * u).astype(np.float32),
        "w2_words": packed_w2[0],
        "w2_scales": packed_w2[1],
        "w3_words": packed_w3[0],
        "w3_scales": packed_w3[1],
        "offs": striped(np.random.permutation(T)[:S]),
        "mix": striped(np.random.permutation(T)[:S]),
        "al": striped8(np.stack([np.random.permutation(S) for _ in range(8)])),
    }


def reference(x_words, x_scales, w1, w2_words, w2_scales, w3_words, w3_scales, offs, mix, al):
    x_mix = unpack_weight(x_words, x_scales)[:, unstriped(mix)]
    e = relu(mxq(f64(w1), 0, "e4m3").T @ x_mix)
    xq = unpack_weight(x_words, x_scales)[:, unstriped(offs)]
    s = unpack_weight(w2_words, w2_scales).T @ xq
    mk = sigmoid(s)
    z = e * (mk[np.arange(H)[:, None], runs(al, H)])
    out_0 = unpack_weight(w3_words, w3_scales).T @ mxq(z, 0, "e4m3")
    return (out_0,) + planes(out_0)

@@ -1,0 +1,182 @@
+from contextlib import ExitStack
+
+import concourse.mybir as mybir
+
+K, T, S, H, N = 512, 2048, 512, 512, 512
+FLOPS = 2 * K * H * S + 2 * K * H * S + 2 * H * N * S
+
+F32 = mybir.dt.float32
+BF16 = mybir.dt.bfloat16
+I32 = mybir.dt.int32
+U32 = mybir.dt.uint32
+U16 = mybir.dt.uint16
+U8 = mybir.dt.uint8
+FP8X4 = mybir.dt.float8_e4m3fn_x4
+ALU = mybir.AluOpType
+ACT = mybir.ActivationFunctionType
+
+P = 128
+PACK = 4
+CHUNK = 128
+LOOKUP = 128
+
+
+def load_scale_rows(queues, plane, rows):
+    for q, queue in enumerate(queues):
+        queue.dma_start(out=plane[32 * q : 32 * q + 4, :].bitcast(I32), in_=rows[4 * q : 4 * q + 4, :].bitcast(I32))
+
+
+def words_of(dram):
+    return dram[0].rearrange("p n t -> p (n t)").bitcast(I32)
+
+
+def deal(nc, dealt, plain):
+    nc.vector.tensor_copy(out=dealt.rearrange("p (t m) -> p m t", t=PACK), in_=plain.rearrange("p (m t) -> p m t", t=PACK))
+
+
+def mx(nc, out, w_words, w_scales, a_words, a_scales):
+    nc.tensor.matmul_mx(out=out, lhsT=w_words.bitcast(FP8X4), lhsT_scale=w_scales, rhs=a_words.bitcast(FP8X4), rhs_scale=a_scales, start=True, stop=True)
+
+
+def tile_picked_maskdec_relu_po_kernel(
+    tc, x_words, x_scales, w1, w2_words, w2_scales, w3_words, w3_scales, offs, mix, al, out_0, out_1, out_2
+):
+    nc = tc.nc
+    chunks = S // CHUNK
+    with ExitStack() as ctx:
+        keep = ctx.enter_context(tc.tile_pool(name="keep", bufs=1))
+        psum = ctx.enter_context(tc.psum_pool(name="psum", bufs=1))
+
+        def tile(name, shape, dtype):
+            return keep.tile(shape, dtype, name=name, align_bytes=64)
+
+        offs_sb = tile("offs_sb", [P, S // 16], U16)
+        mix_sb = tile("mix_sb", [P, S // 16], U16)
+        al_sb = tile("al_sb", [P, S // 16], U16)
+        xw = tile("xw", [P, T], I32)
+        xs = tile("xs", [P, T], U8)
+        w1_raw = tile("w1_raw", [P, PACK, H], F32)
+        w2w_in = tile("w2w_in", [P, H], I32)
+        w2s_in = tile("w2s_in", [P, H], U8)
+
+        nc.vector.memset(xs[:].bitcast(I32), 0)
+        nc.vector.memset(w2s_in[:].bitcast(I32), 0)
+
+        nc.sync.dma_start(out=offs_sb[:], in_=offs)
+        nc.sync.dma_start(out=mix_sb[:], in_=mix)
+        nc.sync.dma_start(out=al_sb[:], in_=al)
+        nc.sync.dma_start(out=w2w_in[:], in_=words_of(w2_words))
+        nc.sync.dma_start(out=xw[:], in_=words_of(x_words))
+        nc.sync.dma_start(out=w1_raw[:], in_=w1.rearrange("(p j) c -> p j c", j=PACK))
+        side_queues = [nc.scalar, nc.scalar, nc.scalar, nc.gpsimd]
+        load_scale_rows(side_queues, xs, x_scales[0])
+        load_scale_rows(side_queues, w2s_in, w2_scales[0])
+
+        qw = tile("qw", [P, S], U32)
+        qs = tile("qs", [P, S], U8)
+        mw = tile("mw", [P, S], U32)
+        ms = tile("ms", [P, S], U8)
+        w2w = tile("w2w", [P, H], I32)
+        w2s = tile("w2s", [P, H], U8)
+        w3w = tile("w3w", [P, N], I32)
+        w3s = tile("w3s", [P, N], U8)
+
+        deal(nc, w2w[:], w2w_in[:])
+        nc.vector.tensor_copy(out=qs[:], in_=xs[:].indirect(offs_sb[:]))
+        deal(nc, w2s[:], w2s_in[:])
+        nc.vector.tensor_copy(out=qw[:], in_=xw[:].bitcast(U32).indirect(offs_sb[:]))
+        nc.sync.dma_start(out=w2w_in[:], in_=words_of(w3_words))
+        load_scale_rows([nc.sync] * 4, w2s_in, w3_scales[0])
+
+        s_sb = []
+        for t in range(PACK):
+            cols = slice(t * P, (t + 1) * P)
+            s_ps = psum.tile([P, S], F32, name=f"s_ps{t}", tag=f"so{t}")
+            mx(nc, s_ps[:], w2w[:, cols], w2s[:, cols], qw[:], qs[:])
+            row = tile(f"s_sb{t}", [P, S], F32)
+            nc.scalar.copy(out=row[:], in_=s_ps[:])
+            s_sb.append(row)
+
+        nc.vector.tensor_copy(out=mw[:], in_=xw[:].bitcast(U32).indirect(mix_sb[:]))
+        nc.vector.tensor_copy(out=ms[:], in_=xs[:].indirect(mix_sb[:]))
+
+        w1_bf = tile("w1_bf", [P, H * PACK], BF16)
+        nc.vector.tensor_copy(
+            out=w1_bf[:].rearrange("p (t m j) -> p m t j", t=PACK, j=PACK),
+            in_=w1_raw[:].rearrange("p j (m t) -> p m t j", t=PACK),
+        )
+        deal(nc, w3w[:], w2w_in[:])
+        w1w = tile("w1w", [P, H], U32)
+        w1s = tile("w1s", [P, H], U8)
+        nc.vector.quantize_mx(out=w1w[:].bitcast(FP8X4), scales=w1s[:], in_=w1_bf[:])
+        deal(nc, w3s[:], w2s_in[:])
+
+        picked = []
+        for g in range(S // LOOKUP):
+            mask = tile(f"mask{g}", [P, PACK, LOOKUP], F32)
+            for t in range(PACK):
+                nc.scalar.activation(
+                    out=mask[:, t, :], in_=s_sb[t][:].indirect(al_sb[:, g * LOOKUP // 16 : (g + 1) * LOOKUP // 16]), func=ACT.Sigmoid
+                )
+            picked.append(mask)
+
+        yw = tile("yw", [P, S], I32)
+        ys = tile("ys", [P, S], U8)
+        out_rows = out_0.rearrange("(p t) n -> p t n", t=PACK)
+        out_words = words_of(out_1)
+        e_ps = []
+        for c in range(chunks):
+            cols = slice(c * CHUNK, (c + 1) * CHUNK)
+            bank = psum.tile([P, PACK, CHUNK], F32, name=f"e_ps{c}")
+            for t in range(PACK):
+                rows = slice(t * P, (t + 1) * P)
+                mx(nc, bank[:, t, :], w1w[:, rows], w1s[:, rows], mw[:, cols], ms[:, cols])
+            e_ps.append(bank)
+
+        z_bf, y_ps, y_bf = {}, {}, {}
+
+        def masked(c):
+            g, first = divmod(c * CHUNK, LOOKUP)
+            z_bf[c] = tile(f"z_bf{c}", [P, CHUNK, PACK], BF16)
+            nc.vector.scalar_tensor_tensor(
+                out=z_bf[c][:],
+                in0=e_ps[c][:].rearrange("p t n -> p n t"),
+                scalar=0.0,
+                in1=picked[g][:, :, first : first + CHUNK].rearrange("p t n -> p n t"),
+                op0=ALU.max,
+                op1=ALU.mult,
+            )
+
+        def decode(c):
+            zw = tile(f"zw{c}", [P, CHUNK], U32)
+            zs = tile(f"zs{c}", [P, CHUNK], U8)
+            nc.vector.quantize_mx(out=zw[:].bitcast(FP8X4), scales=zs[:], in_=z_bf[c][:].rearrange("p n t -> p (n t)"))
+            y_ps[c] = psum.tile([P, PACK, CHUNK], F32, name=f"y_ps{c}", tag=f"so{c}")
+            for t in range(PACK):
+                rows = slice(t * P, (t + 1) * P)
+                mx(nc, y_ps[c][:, t, :], w3w[:, rows], w3s[:, rows], zw[:], zs[:])
+
+        def leave(c):
+            cols = slice(c * CHUNK, (c + 1) * CHUNK)
+            y = tile(f"y{c}", [P, PACK, CHUNK], F32)
+            nc.scalar.copy(out=y[:], in_=y_ps[c][:])
+            nc.sync.dma_start(out=out_rows[:, :, cols], in_=y[:])
+            y_bf[c] = tile(f"y_bf{c}", [P, CHUNK, PACK], BF16)
+            nc.vector.tensor_copy(
+                out=y_bf[c][:].rearrange("p (b i) t -> p b t i", i=4), in_=y[:].rearrange("p t (b i) -> p b t i", i=4)
+            )
+
+        def planes(c):
+            cols = slice(c * CHUNK, (c + 1) * CHUNK)
+            nc.vector.quantize_mx(out=yw[:, cols].bitcast(FP8X4), scales=ys[:, cols], in_=y_bf[c][:].rearrange("p n t -> p (n t)"))
+            nc.sync.dma_start(out=out_words[:, cols], in_=yw[:, cols])
+
+        stages = [masked, decode, leave, planes]
+        for step in range(chunks + len(stages) - 1):
+            for lag, stage in enumerate(stages):
+                if 0 <= step - lag < chunks:
+                    stage(step - lag)
+
+        for q in range(4):
+            queue = nc.sync if q % 2 == 0 else nc.scalar
+            queue.dma_start(out=out_2[0][4 * q : 4 * q + 4, :].bitcast(I32), in_=ys[32 * q : 32 * q + 4, :].bitcast(I32))

@@ -19,6 +19,8 @@ P = 128
 PACK = 4
 CHUNK = 128
 LOOKUP = 128
+ON_VECTOR = 1
+HALF = S // 2
 
 
 def load_scale_rows(queues, plane, rows):
@@ -47,8 +49,8 @@ def tile_picked_maskdec_relu_po_kernel(
         keep = ctx.enter_context(tc.tile_pool(name="keep", bufs=1))
         psum = ctx.enter_context(tc.psum_pool(name="psum", bufs=1))
 
-        def tile(name, shape, dtype):
-            return keep.tile(shape, dtype, name=name, align_bytes=64)
+        def tile(name, shape, dtype, tag=None):
+            return keep.tile(shape, dtype, name=name, tag=tag or name, align_bytes=64)
 
         offs_sb = tile("offs_sb", [P, S // 16], U16)
         mix_sb = tile("mix_sb", [P, S // 16], U16)
@@ -57,24 +59,27 @@ def tile_picked_maskdec_relu_po_kernel(
         xs = tile("xs", [P, T], U8)
         w1_raw = tile("w1_raw", [P, PACK, H], F32)
         w2w_in = tile("w2w_in", [P, H], I32)
-        w2s_in = tile("w2s_in", [P, H], U8)
+        w2s_in = tile("w2s_in", [P, H], U8, tag="shared")
+        w3w_in = tile("w3w_in", [P, N], I32)
+        w3s_in = tile("w3s_in", [P, N], U8)
 
-        nc.vector.memset(xs[:].bitcast(I32), 0)
+        nc.vector.memset(xs[:, : T // 2].bitcast(I32), 0)
+        nc.gpsimd.memset(xs[:, T // 2 :].bitcast(I32), 0)
         nc.vector.memset(w2s_in[:].bitcast(I32), 0)
+        nc.vector.memset(w3s_in[:].bitcast(I32), 0)
 
         nc.sync.dma_start(out=offs_sb[:], in_=offs)
         nc.sync.dma_start(out=mix_sb[:], in_=mix)
-        nc.sync.dma_start(out=al_sb[:], in_=al)
         nc.sync.dma_start(out=w2w_in[:], in_=words_of(w2_words))
+        load_scale_rows([nc.sync, nc.scalar] * 2, xs, x_scales[0])
         nc.sync.dma_start(out=xw[:], in_=words_of(x_words))
+        load_scale_rows([nc.sync] * 4, w2s_in, w2_scales[0])
         nc.sync.dma_start(out=w1_raw[:], in_=w1.rearrange("(p j) c -> p j c", j=PACK))
-        side_queues = [nc.scalar, nc.scalar, nc.scalar, nc.gpsimd]
-        load_scale_rows(side_queues, xs, x_scales[0])
-        load_scale_rows(side_queues, w2s_in, w2_scales[0])
+        nc.sync.dma_start(out=al_sb[:], in_=al)
+        nc.sync.dma_start(out=w3w_in[:], in_=words_of(w3_words))
+        load_scale_rows([nc.sync] * 4, w3s_in, w3_scales[0])
 
-        qw = tile("qw", [P, S], U32)
         qs = tile("qs", [P, S], U8)
-        mw = tile("mw", [P, S], U32)
         ms = tile("ms", [P, S], U8)
         w2w = tile("w2w", [P, H], I32)
         w2s = tile("w2s", [P, H], U8)
@@ -83,41 +88,46 @@ def tile_picked_maskdec_relu_po_kernel(
 
         deal(nc, w2w[:], w2w_in[:])
         nc.vector.tensor_copy(out=qs[:], in_=xs[:].indirect(offs_sb[:]))
-        deal(nc, w2s[:], w2s_in[:])
-        nc.vector.tensor_copy(out=qw[:], in_=xw[:].bitcast(U32).indirect(offs_sb[:]))
-        nc.sync.dma_start(out=w2w_in[:], in_=words_of(w3_words))
-        load_scale_rows([nc.sync] * 4, w2s_in, w3_scales[0])
-
-        s_sb = []
-        for t in range(PACK):
-            cols = slice(t * P, (t + 1) * P)
-            s_ps = psum.tile([P, S], F32, name=f"s_ps{t}", tag=f"so{t}")
-            mx(nc, s_ps[:], w2w[:, cols], w2s[:, cols], qw[:], qs[:])
-            row = tile(f"s_sb{t}", [P, S], F32)
-            nc.scalar.copy(out=row[:], in_=s_ps[:])
-            s_sb.append(row)
-
-        nc.vector.tensor_copy(out=mw[:], in_=xw[:].bitcast(U32).indirect(mix_sb[:]))
         nc.vector.tensor_copy(out=ms[:], in_=xs[:].indirect(mix_sb[:]))
+        deal(nc, w2s[:], w2s_in[:])
+
+        s_sb = [tile(f"s_sb{t}", [P, S], F32) for t in range(PACK)]
+        for h in range(2):
+            half = slice(h * HALF, (h + 1) * HALF)
+            qw = tile(f"qw{h}", [P, HALF], U32)
+            nc.vector.tensor_copy(out=qw[:], in_=xw[:].bitcast(U32).indirect(offs_sb[:, h * HALF // 16 : (h + 1) * HALF // 16]))
+            for t in range(PACK):
+                rows = slice(t * P, (t + 1) * P)
+                s_ps = psum.tile([P, HALF], F32, name=f"s_ps{h}{t}", tag=f"bank{h * PACK + t}")
+                mx(nc, s_ps[:], w2w[:, rows], w2s[:, rows], qw[:], qs[:, half])
+                if t < ON_VECTOR:
+                    nc.scalar.activation(out=s_sb[t][:, half], in_=s_ps[:], func=ACT.Sigmoid)
+                else:
+                    nc.scalar.copy(out=s_sb[t][:, half], in_=s_ps[:])
+
+        mw = tile("mw", [P, S], U32, tag="shared")
+        nc.vector.tensor_copy(out=mw[:], in_=xw[:].bitcast(U32).indirect(mix_sb[:]))
 
         w1_bf = tile("w1_bf", [P, H * PACK], BF16)
         nc.vector.tensor_copy(
             out=w1_bf[:].rearrange("p (t m j) -> p m t j", t=PACK, j=PACK),
             in_=w1_raw[:].rearrange("p j (m t) -> p m t j", t=PACK),
         )
-        deal(nc, w3w[:], w2w_in[:])
+        deal(nc, w3w[:], w3w_in[:])
         w1w = tile("w1w", [P, H], U32)
         w1s = tile("w1s", [P, H], U8)
         nc.vector.quantize_mx(out=w1w[:].bitcast(FP8X4), scales=w1s[:], in_=w1_bf[:])
-        deal(nc, w3s[:], w2s_in[:])
+        deal(nc, w3s[:], w3s_in[:])
 
         picked = []
         for g in range(S // LOOKUP):
             mask = tile(f"mask{g}", [P, PACK, LOOKUP], F32)
             for t in range(PACK):
-                nc.scalar.activation(
-                    out=mask[:, t, :], in_=s_sb[t][:].indirect(al_sb[:, g * LOOKUP // 16 : (g + 1) * LOOKUP // 16]), func=ACT.Sigmoid
-                )
+                looked_up = s_sb[t][:].indirect(al_sb[:, g * LOOKUP // 16 : (g + 1) * LOOKUP // 16])
+                if t < ON_VECTOR:
+                    nc.vector.tensor_copy(out=mask[:, t, :], in_=looked_up)
+                else:
+                    nc.scalar.activation(out=mask[:, t, :], in_=looked_up, func=ACT.Sigmoid)
             picked.append(mask)
 
         yw = tile("yw", [P, S], I32)
@@ -127,7 +137,7 @@ def tile_picked_maskdec_relu_po_kernel(
         e_ps = []
         for c in range(chunks):
             cols = slice(c * CHUNK, (c + 1) * CHUNK)
-            bank = psum.tile([P, PACK, CHUNK], F32, name=f"e_ps{c}")
+            bank = psum.tile([P, PACK, CHUNK], F32, name=f"e_ps{c}", tag=f"bank{c}")
             for t in range(PACK):
                 rows = slice(t * P, (t + 1) * P)
                 mx(nc, bank[:, t, :], w1w[:, rows], w1s[:, rows], mw[:, cols], ms[:, cols])
@@ -151,7 +161,7 @@ def tile_picked_maskdec_relu_po_kernel(
             zw = tile(f"zw{c}", [P, CHUNK], U32)
             zs = tile(f"zs{c}", [P, CHUNK], U8)
             nc.vector.quantize_mx(out=zw[:].bitcast(FP8X4), scales=zs[:], in_=z_bf[c][:].rearrange("p n t -> p (n t)"))
-            y_ps[c] = psum.tile([P, PACK, CHUNK], F32, name=f"y_ps{c}", tag=f"so{c}")
+            y_ps[c] = psum.tile([P, PACK, CHUNK], F32, name=f"y_ps{c}", tag=f"bank{PACK + c}")
             for t in range(PACK):
                 rows = slice(t * P, (t + 1) * P)
                 mx(nc, y_ps[c][:, t, :], w3w[:, rows], w3s[:, rows], zw[:], zs[:])
@@ -159,12 +169,18 @@ def tile_picked_maskdec_relu_po_kernel(
         def leave(c):
             cols = slice(c * CHUNK, (c + 1) * CHUNK)
             y = tile(f"y{c}", [P, PACK, CHUNK], F32)
-            nc.scalar.copy(out=y[:], in_=y_ps[c][:])
-            nc.sync.dma_start(out=out_rows[:, :, cols], in_=y[:])
             y_bf[c] = tile(f"y_bf{c}", [P, CHUNK, PACK], BF16)
-            nc.vector.tensor_copy(
-                out=y_bf[c][:].rearrange("p (b i) t -> p b t i", i=4), in_=y[:].rearrange("p t (b i) -> p b t i", i=4)
-            )
+            if c == chunks - 1:
+                nc.vector.tensor_copy(out=y_bf[c][:], in_=y_ps[c][:].rearrange("p t n -> p n t"))
+                for pair in (slice(0, 2), slice(2, 4)):
+                    nc.scalar.copy(out=y[:, pair, :], in_=y_ps[c][:, pair, :])
+                    nc.sync.dma_start(out=out_rows[:, pair, cols], in_=y[:, pair, :])
+            else:
+                nc.scalar.copy(out=y[:], in_=y_ps[c][:])
+                nc.sync.dma_start(out=out_rows[:, :, cols], in_=y[:])
+                nc.vector.tensor_copy(
+                    out=y_bf[c][:].rearrange("p (b i) t -> p b t i", i=4), in_=y[:].rearrange("p t (b i) -> p b t i", i=4)
+                )
 
         def planes(c):
             cols = slice(c * CHUNK, (c + 1) * CHUNK)

@@ -47,6 +47,7 @@ def tile_picked_maskdec_relu_po_kernel(
     chunks = S // CHUNK
     with ExitStack() as ctx:
         keep = ctx.enter_context(tc.tile_pool(name="keep", bufs=1))
+        stage = ctx.enter_context(tc.tile_pool(name="stage", bufs=1))
         psum = ctx.enter_context(tc.psum_pool(name="psum", bufs=1))
 
         def tile(name, shape, dtype, tag=None):
@@ -59,7 +60,7 @@ def tile_picked_maskdec_relu_po_kernel(
         xs = tile("xs", [P, T], U8)
         w1_raw = tile("w1_raw", [P, PACK, H], F32)
         w2w_in = tile("w2w_in", [P, H], I32)
-        w2s_in = tile("w2s_in", [P, H], U8, tag="shared")
+        w2s_in = stage.tile([P, H], U8, name="w2s_in", align_bytes=64, offset=4 * HALF - H // 2)
         w3w_in = tile("w3w_in", [P, N], I32)
         w3s_in = tile("w3s_in", [P, N], U8)
 
@@ -94,7 +95,10 @@ def tile_picked_maskdec_relu_po_kernel(
         s_sb = [tile(f"s_sb{t}", [P, S], F32) for t in range(PACK)]
         for h in range(2):
             half = slice(h * HALF, (h + 1) * HALF)
-            qw = tile(f"qw{h}", [P, HALF], U32)
+            if h == 0:
+                qw = tile("qw0", [P, HALF], U32)
+            else:
+                qw = stage.tile([P, HALF], U32, name="qw1", align_bytes=64, offset=0)
             nc.vector.tensor_copy(out=qw[:], in_=xw[:].bitcast(U32).indirect(offs_sb[:, h * HALF // 16 : (h + 1) * HALF // 16]))
             for t in range(PACK):
                 rows = slice(t * P, (t + 1) * P)
@@ -105,7 +109,7 @@ def tile_picked_maskdec_relu_po_kernel(
                 else:
                     nc.scalar.copy(out=s_sb[t][:, half], in_=s_ps[:])
 
-        mw = tile("mw", [P, S], U32, tag="shared")
+        mw = stage.tile([P, S], U32, name="mw", align_bytes=64, offset=4 * HALF)
         nc.vector.tensor_copy(out=mw[:], in_=xw[:].bitcast(U32).indirect(mix_sb[:]))
 
         w1_bf = tile("w1_bf", [P, H * PACK], BF16)
@@ -161,31 +165,37 @@ def tile_picked_maskdec_relu_po_kernel(
             zw = tile(f"zw{c}", [P, CHUNK], U32)
             zs = tile(f"zs{c}", [P, CHUNK], U8)
             nc.vector.quantize_mx(out=zw[:].bitcast(FP8X4), scales=zs[:], in_=z_bf[c][:].rearrange("p n t -> p (n t)"))
-            y_ps[c] = psum.tile([P, PACK, CHUNK], F32, name=f"y_ps{c}", tag=f"bank{PACK + c}")
+            if c == chunks - 1:
+                y_ps[c] = [psum.tile([P, 2, CHUNK], F32, name=f"y_ps{c}{u}", tag=f"bank{(PACK + c + u) % 8}") for u in range(2)]
+            else:
+                bank = psum.tile([P, PACK, CHUNK], F32, name=f"y_ps{c}", tag=f"bank{PACK + c}")
+                y_ps[c] = [bank[:, 0:2, :], bank[:, 2:4, :], bank]
             for t in range(PACK):
                 rows = slice(t * P, (t + 1) * P)
-                mx(nc, y_ps[c][:, t, :], w3w[:, rows], w3s[:, rows], zw[:], zs[:])
+                mx(nc, y_ps[c][t // 2][:, t % 2, :], w3w[:, rows], w3s[:, rows], zw[:], zs[:])
 
         def leave(c):
             cols = slice(c * CHUNK, (c + 1) * CHUNK)
             y = tile(f"y{c}", [P, PACK, CHUNK], F32)
             y_bf[c] = tile(f"y_bf{c}", [P, CHUNK, PACK], BF16)
             if c == chunks - 1:
-                nc.vector.tensor_copy(out=y_bf[c][:], in_=y_ps[c][:].rearrange("p t n -> p n t"))
-                for pair in (slice(0, 2), slice(2, 4)):
-                    nc.scalar.copy(out=y[:, pair, :], in_=y_ps[c][:, pair, :])
+                for u in range(2):
+                    pair = slice(2 * u, 2 * u + 2)
+                    nc.scalar.copy(out=y[:, pair, :], in_=y_ps[c][u][:])
                     nc.sync.dma_start(out=out_rows[:, pair, cols], in_=y[:, pair, :])
             else:
-                nc.scalar.copy(out=y[:], in_=y_ps[c][:])
+                nc.scalar.copy(out=y[:], in_=y_ps[c][2][:])
                 nc.sync.dma_start(out=out_rows[:, :, cols], in_=y[:])
-                nc.vector.tensor_copy(
-                    out=y_bf[c][:].rearrange("p (b i) t -> p b t i", i=4), in_=y[:].rearrange("p t (b i) -> p b t i", i=4)
-                )
+            nc.vector.tensor_copy(
+                out=y_bf[c][:].rearrange("p (b i) t -> p b t i", i=4), in_=y[:].rearrange("p t (b i) -> p b t i", i=4)
+            )
 
         def planes(c):
             cols = slice(c * CHUNK, (c + 1) * CHUNK)
             nc.vector.quantize_mx(out=yw[:, cols].bitcast(FP8X4), scales=ys[:, cols], in_=y_bf[c][:].rearrange("p n t -> p (n t)"))
-            nc.sync.dma_start(out=out_words[:, cols], in_=yw[:, cols])
+            if c % 2 == 1:
+                pair = slice((c - 1) * CHUNK, (c + 1) * CHUNK)
+                nc.sync.dma_start(out=out_words[:, pair], in_=yw[:, pair])
 
         stages = [masked, decode, leave, planes]
         for step in range(chunks + len(stages) - 1):

@@ -18,7 +18,7 @@ ACT = mybir.ActivationFunctionType
 P = 128
 PACK = 4
 CHUNK = 128
-LOOKUP = 128
+LOOKUP = 256
 ON_VECTOR = 1
 HALF = S // 2
 
@@ -123,16 +123,19 @@ def tile_picked_maskdec_relu_po_kernel(
         nc.vector.quantize_mx(out=w1w[:].bitcast(FP8X4), scales=w1s[:], in_=w1_bf[:])
         deal(nc, w3s[:], w3s_in[:])
 
-        picked = []
+        picked = [tile(f"mask{g}", [P, PACK, LOOKUP], F32) for g in range(S // LOOKUP)]
+
+        def window(g, t):
+            return s_sb[t][:].indirect(al_sb[:, g * LOOKUP // 16 : (g + 1) * LOOKUP // 16])
+
+        def look_up_on_vector(g):
+            for t in range(ON_VECTOR):
+                nc.vector.tensor_copy(out=picked[g][:, t, :], in_=window(g, t))
+
         for g in range(S // LOOKUP):
-            mask = tile(f"mask{g}", [P, PACK, LOOKUP], F32)
-            for t in range(PACK):
-                looked_up = s_sb[t][:].indirect(al_sb[:, g * LOOKUP // 16 : (g + 1) * LOOKUP // 16])
-                if t < ON_VECTOR:
-                    nc.vector.tensor_copy(out=mask[:, t, :], in_=looked_up)
-                else:
-                    nc.scalar.activation(out=mask[:, t, :], in_=looked_up, func=ACT.Sigmoid)
-            picked.append(mask)
+            for t in range(ON_VECTOR, PACK):
+                nc.scalar.activation(out=picked[g][:, t, :], in_=window(g, t), func=ACT.Sigmoid)
+        look_up_on_vector(0)
 
         yw = tile("yw", [P, S], I32)
         ys = tile("ys", [P, S], U8)
@@ -147,7 +150,7 @@ def tile_picked_maskdec_relu_po_kernel(
                 mx(nc, bank[:, t, :], w1w[:, rows], w1s[:, rows], mw[:, cols], ms[:, cols])
             e_ps.append(bank)
 
-        z_bf, y_ps, y_bf = {}, {}, {}
+        z_bf, y_ps, y_sb, y_bf = {}, {}, {}, {}
 
         def masked(c):
             g, first = divmod(c * CHUNK, LOOKUP)
@@ -186,8 +189,11 @@ def tile_picked_maskdec_relu_po_kernel(
             else:
                 nc.scalar.copy(out=y[:], in_=y_ps[c][2][:])
                 nc.sync.dma_start(out=out_rows[:, :, cols], in_=y[:])
+            y_sb[c] = y
+
+        def interleave(c):
             nc.vector.tensor_copy(
-                out=y_bf[c][:].rearrange("p (b i) t -> p b t i", i=4), in_=y[:].rearrange("p t (b i) -> p b t i", i=4)
+                out=y_bf[c][:].rearrange("p (b i) t -> p b t i", i=4), in_=y_sb[c][:].rearrange("p t (b i) -> p b t i", i=4)
             )
 
         def planes(c):
@@ -197,11 +203,27 @@ def tile_picked_maskdec_relu_po_kernel(
                 pair = slice((c - 1) * CHUNK, (c + 1) * CHUNK)
                 nc.sync.dma_start(out=out_words[:, pair], in_=yw[:, pair])
 
-        stages = [masked, decode, leave, planes]
-        for step in range(chunks + len(stages) - 1):
-            for lag, stage in enumerate(stages):
-                if 0 <= step - lag < chunks:
-                    stage(step - lag)
+        masked(0)
+        masked(1)
+        decode(0)
+        look_up_on_vector(1)
+        decode(1)
+        masked(2)
+        leave(0)
+        leave(1)
+        masked(3)
+        decode(2)
+        interleave(0)
+        decode(3)
+        leave(2)
+        leave(3)
+        interleave(1)
+        planes(0)
+        planes(1)
+        interleave(2)
+        interleave(3)
+        planes(2)
+        planes(3)
 
         for q in range(4):
             queue = nc.sync if q % 2 == 0 else nc.scalar

@@ -19,6 +19,7 @@ P = 128
 PACK = 4
 CHUNK = 128
 LOOKUP = 256
+PIECES = ((0, 128), (128, 128), (256, 128), (384, 64), (448, 64))
 ON_VECTOR = 1
 HALF = S // 2
 
@@ -150,58 +151,54 @@ def tile_picked_maskdec_relu_po_kernel(
                 mx(nc, bank[:, t, :], w1w[:, rows], w1s[:, rows], mw[:, cols], ms[:, cols])
             e_ps.append(bank)
 
+        y = [tile(f"y{chunk}", [P, PACK, CHUNK], F32) for chunk in range(chunks)]
         z_bf, y_ps, y_sb, y_bf = {}, {}, {}, {}
 
         def masked(c):
-            g, first = divmod(c * CHUNK, LOOKUP)
-            z_bf[c] = tile(f"z_bf{c}", [P, CHUNK, PACK], BF16)
+            first, width = PIECES[c]
+            in_bank = slice(first % CHUNK, first % CHUNK + width)
+            in_group = slice(first % LOOKUP, first % LOOKUP + width)
+            z_bf[c] = tile(f"z_bf{c}", [P, width, PACK], BF16)
             nc.vector.scalar_tensor_tensor(
                 out=z_bf[c][:],
-                in0=e_ps[c][:].rearrange("p t n -> p n t"),
+                in0=e_ps[first // CHUNK][:, :, in_bank].rearrange("p t n -> p n t"),
                 scalar=0.0,
-                in1=picked[g][:, :, first : first + CHUNK].rearrange("p t n -> p n t"),
+                in1=picked[first // LOOKUP][:, :, in_group].rearrange("p t n -> p n t"),
                 op0=ALU.max,
                 op1=ALU.mult,
             )
 
         def decode(c):
-            zw = tile(f"zw{c}", [P, CHUNK], U32)
-            zs = tile(f"zs{c}", [P, CHUNK], U8)
+            width = PIECES[c][1]
+            zw = tile(f"zw{c}", [P, width], U32)
+            zs = tile(f"zs{c}", [P, width], U8)
             nc.vector.quantize_mx(out=zw[:].bitcast(FP8X4), scales=zs[:], in_=z_bf[c][:].rearrange("p n t -> p (n t)"))
-            if c == chunks - 1:
-                y_ps[c] = [psum.tile([P, 2, CHUNK], F32, name=f"y_ps{c}{u}", tag=f"bank{(PACK + c + u) % 8}") for u in range(2)]
-            else:
-                bank = psum.tile([P, PACK, CHUNK], F32, name=f"y_ps{c}", tag=f"bank{PACK + c}")
-                y_ps[c] = [bank[:, 0:2, :], bank[:, 2:4, :], bank]
+            y_ps[c] = psum.tile([P, PACK, width], F32, name=f"y_ps{c}", tag=f"bank{(PACK + c) % 8}")
             for t in range(PACK):
                 rows = slice(t * P, (t + 1) * P)
-                mx(nc, y_ps[c][t // 2][:, t % 2, :], w3w[:, rows], w3s[:, rows], zw[:], zs[:])
+                mx(nc, y_ps[c][:, t, :], w3w[:, rows], w3s[:, rows], zw[:], zs[:])
 
         def leave(c):
-            cols = slice(c * CHUNK, (c + 1) * CHUNK)
-            y = tile(f"y{c}", [P, PACK, CHUNK], F32)
-            y_bf[c] = tile(f"y_bf{c}", [P, CHUNK, PACK], BF16)
-            if c == chunks - 1:
-                for u in range(2):
-                    pair = slice(2 * u, 2 * u + 2)
-                    nc.scalar.copy(out=y[:, pair, :], in_=y_ps[c][u][:])
-                    nc.sync.dma_start(out=out_rows[:, pair, cols], in_=y[:, pair, :])
-            else:
-                nc.scalar.copy(out=y[:], in_=y_ps[c][2][:])
-                nc.sync.dma_start(out=out_rows[:, :, cols], in_=y[:])
-            y_sb[c] = y
+            first, width = PIECES[c]
+            chunk = first // CHUNK
+            y_sb[c] = y[chunk][:, :, first % CHUNK : first % CHUNK + width]
+            nc.scalar.copy(out=y_sb[c], in_=y_ps[c][:])
+            if (first + width) % CHUNK == 0:
+                nc.sync.dma_start(out=out_rows[:, :, chunk * CHUNK : (chunk + 1) * CHUNK], in_=y[chunk][:])
 
         def interleave(c):
+            y_bf[c] = tile(f"y_bf{c}", [P, PIECES[c][1], PACK], BF16)
             nc.vector.tensor_copy(
-                out=y_bf[c][:].rearrange("p (b i) t -> p b t i", i=4), in_=y_sb[c][:].rearrange("p t (b i) -> p b t i", i=4)
+                out=y_bf[c][:].rearrange("p (b i) t -> p b t i", i=4), in_=y_sb[c].rearrange("p t (b i) -> p b t i", i=4)
             )
 
         def planes(c):
-            cols = slice(c * CHUNK, (c + 1) * CHUNK)
+            first, width = PIECES[c]
+            cols = slice(first, first + width)
             nc.vector.quantize_mx(out=yw[:, cols].bitcast(FP8X4), scales=ys[:, cols], in_=y_bf[c][:].rearrange("p n t -> p (n t)"))
-            if c % 2 == 1:
-                pair = slice((c - 1) * CHUNK, (c + 1) * CHUNK)
-                nc.sync.dma_start(out=out_words[:, pair], in_=yw[:, pair])
+            if (first + width) % HALF == 0:
+                half = slice(first + width - HALF, first + width)
+                nc.sync.dma_start(out=out_words[:, half], in_=yw[:, half])
 
         masked(0)
         masked(1)
@@ -213,17 +210,22 @@ def tile_picked_maskdec_relu_po_kernel(
         leave(1)
         masked(3)
         decode(2)
-        interleave(0)
+        masked(4)
         decode(3)
+        interleave(0)
+        decode(4)
         leave(2)
         leave(3)
+        leave(4)
         interleave(1)
         planes(0)
         planes(1)
         interleave(2)
         interleave(3)
         planes(2)
+        interleave(4)
         planes(3)
+        planes(4)
 
         for q in range(4):
             queue = nc.sync if q % 2 == 0 else nc.scalar

@@ -65,8 +65,7 @@ def tile_picked_maskdec_relu_po_kernel(
         w3w_in = tile("w3w_in", [P, N], I32)
         w3s_in = tile("w3s_in", [P, N], U8)
 
-        nc.vector.memset(xs[:, : T // 2].bitcast(I32), 0)
-        nc.gpsimd.memset(xs[:, T // 2 :].bitcast(I32), 0)
+        nc.vector.memset(xs[:].bitcast(I32), 0)
         nc.vector.memset(w2s_in[:].bitcast(I32), 0)
         nc.vector.memset(w3s_in[:].bitcast(I32), 0)
 
@@ -196,9 +195,10 @@ def tile_picked_maskdec_relu_po_kernel(
             first, width = PIECES[c]
             cols = slice(first, first + width)
             nc.vector.quantize_mx(out=yw[:, cols].bitcast(FP8X4), scales=ys[:, cols], in_=y_bf[c][:].rearrange("p n t -> p (n t)"))
-            if (first + width) % HALF == 0:
-                half = slice(first + width - HALF, first + width)
-                nc.sync.dma_start(out=out_words[:, half], in_=yw[:, half])
+
+        def store_words(queue, first, last):
+            cols = slice(PIECES[first][0], sum(PIECES[last]))
+            queue.dma_start(out=out_words[:, cols], in_=yw[:, cols])
 
         masked(0)
         masked(1)
@@ -223,9 +223,11 @@ def tile_picked_maskdec_relu_po_kernel(
         interleave(2)
         interleave(3)
         planes(2)
+        store_words(nc.sync, 0, 2)
         interleave(4)
         planes(3)
         planes(4)
+        store_words(nc.scalar, 3, 4)
 
         for q in range(4):
             queue = nc.sync if q % 2 == 0 else nc.scalar

@@ -25,8 +25,8 @@ HALF = S // 2
 
 
 def load_scale_rows(queues, plane, rows):
-    for q, queue in enumerate(queues):
-        queue.dma_start(out=plane[32 * q : 32 * q + 4, :].bitcast(I32), in_=rows[4 * q : 4 * q + 4, :].bitcast(I32))
+    for r, queue in enumerate(queues):
+        queue.dma_start(out=plane[r:P:32, :].bitcast(I32), in_=rows[r:16:4, :].bitcast(I32))
 
 
 def words_of(dram):
@@ -114,8 +114,8 @@ def tile_picked_maskdec_relu_po_kernel(
 
         w1_bf = tile("w1_bf", [P, H * PACK], BF16)
         nc.vector.tensor_copy(
-            out=w1_bf[:].rearrange("p (t m j) -> p m t j", t=PACK, j=PACK),
-            in_=w1_raw[:].rearrange("p j (m t) -> p m t j", t=PACK),
+            out=w1_bf[:].rearrange("p (t m j) -> p m j t", t=PACK, j=PACK),
+            in_=w1_raw[:].rearrange("p j (m t) -> p m j t", t=PACK),
         )
         deal(nc, w3w[:], w3w_in[:])
         w1w = tile("w1w", [P, H], U32)

@@ -21,6 +21,7 @@ CHUNK = 128
 LOOKUP = 256
 PIECES = ((0, 128), (128, 128), (256, 128), (384, 64), (448, 64))
 ON_VECTOR = 1
+ON_SCALAR = ((0, 256), (256, 128), (384, 128))
 HALF = S // 2
 
 
@@ -125,16 +126,17 @@ def tile_picked_maskdec_relu_po_kernel(
 
         picked = [tile(f"mask{g}", [P, PACK, LOOKUP], F32) for g in range(S // LOOKUP)]
 
-        def window(g, t):
-            return s_sb[t][:].indirect(al_sb[:, g * LOOKUP // 16 : (g + 1) * LOOKUP // 16])
+        def window(t, first, width):
+            return s_sb[t][:].indirect(al_sb[:, first // 16 : (first + width) // 16])
 
         def look_up_on_vector(g):
             for t in range(ON_VECTOR):
-                nc.vector.tensor_copy(out=picked[g][:, t, :], in_=window(g, t))
+                nc.vector.tensor_copy(out=picked[g][:, t, :], in_=window(t, g * LOOKUP, LOOKUP))
 
-        for g in range(S // LOOKUP):
+        for first, width in ON_SCALAR:
             for t in range(ON_VECTOR, PACK):
-                nc.scalar.activation(out=picked[g][:, t, :], in_=window(g, t), func=ACT.Sigmoid)
+                out = picked[first // LOOKUP][:, t, first % LOOKUP : first % LOOKUP + width]
+                nc.scalar.activation(out=out, in_=window(t, first, width), func=ACT.Sigmoid)
         look_up_on_vector(0)
 
         yw = tile("yw", [P, S], I32)
@@ -220,15 +222,14 @@ def tile_picked_maskdec_relu_po_kernel(
         interleave(1)
         planes(0)
         planes(1)
+        store_words(nc.sync, 0, 1)
         interleave(2)
         interleave(3)
         planes(2)
-        store_words(nc.sync, 0, 2)
         interleave(4)
         planes(3)
         planes(4)
-        store_words(nc.scalar, 3, 4)
+        store_words(nc.scalar, 2, 4)
 
-        for q in range(4):
-            queue = nc.sync if q % 2 == 0 else nc.scalar
-            queue.dma_start(out=out_2[0][4 * q : 4 * q + 4, :].bitcast(I32), in_=ys[32 * q : 32 * q + 4, :].bitcast(I32))
+        for r, queue in enumerate((nc.sync, nc.sync, nc.scalar, nc.sync)):
+            queue.dma_start(out=out_2[0][r:16:4, :].bitcast(I32), in_=ys[r:P:32, :].bitcast(I32))

@@ -38,6 +38,10 @@ def deal(nc, dealt, plain):
     nc.vector.tensor_copy(out=dealt.rearrange("p (t m) -> p m t", t=PACK), in_=plain.rearrange("p (m t) -> p m t", t=PACK))
 
 
+def deal_bytes(nc, dealt, plain):
+    nc.vector.tensor_copy(out=dealt.rearrange("p (t m) -> p t m", t=PACK), in_=plain.rearrange("p (m t) -> p t m", t=PACK))
+
+
 def mx(nc, out, w_words, w_scales, a_words, a_scales):
     nc.tensor.matmul_mx(out=out, lhsT=w_words.bitcast(FP8X4), lhsT_scale=w_scales, rhs=a_words.bitcast(FP8X4), rhs_scale=a_scales, start=True, stop=True)
 
@@ -91,7 +95,7 @@ def tile_picked_maskdec_relu_po_kernel(
         deal(nc, w2w[:], w2w_in[:])
         nc.vector.tensor_copy(out=qs[:], in_=xs[:].indirect(offs_sb[:]))
         nc.vector.tensor_copy(out=ms[:], in_=xs[:].indirect(mix_sb[:]))
-        deal(nc, w2s[:], w2s_in[:])
+        deal_bytes(nc, w2s[:], w2s_in[:])
 
         s_sb = [tile(f"s_sb{t}", [P, S], F32) for t in range(PACK)]
         for h in range(2):
@@ -122,7 +126,7 @@ def tile_picked_maskdec_relu_po_kernel(
         w1w = tile("w1w", [P, H], U32)
         w1s = tile("w1s", [P, H], U8)
         nc.vector.quantize_mx(out=w1w[:].bitcast(FP8X4), scales=w1s[:], in_=w1_bf[:])
-        deal(nc, w3s[:], w3s_in[:])
+        deal_bytes(nc, w3s[:], w3s_in[:])
 
         picked = [tile(f"mask{g}", [P, PACK, LOOKUP], F32) for g in range(S // LOOKUP)]
 

@@ -23,6 +23,8 @@ PIECES = ((0, 128), (128, 128), (256, 128), (384, 64), (448, 64))
 ON_VECTOR = 1
 ON_SCALAR = ((0, 256), (256, 128), (384, 128))
 HALF = S // 2
+E_BANKS = 3
+ROUNDED_AT = 4096
 
 
 def load_scale_rows(queues, plane, rows):
@@ -40,6 +42,10 @@ def deal(nc, dealt, plain):
 
 def deal_bytes(nc, dealt, plain):
     nc.vector.tensor_copy(out=dealt.rearrange("p (t m) -> p t m", t=PACK), in_=plain.rearrange("p (m t) -> p t m", t=PACK))
+
+
+def deal_on_gpsimd(nc, dealt, plain):
+    nc.gpsimd.tensor_copy(out=dealt.rearrange("p (t m) -> p t m", t=PACK), in_=plain.rearrange("p (m t) -> p t m", t=PACK))
 
 
 def mx(nc, out, w_words, w_scales, a_words, a_scales):
@@ -89,8 +95,6 @@ def tile_picked_maskdec_relu_po_kernel(
         ms = tile("ms", [P, S], U8)
         w2w = tile("w2w", [P, H], I32)
         w2s = tile("w2s", [P, H], U8)
-        w3w = tile("w3w", [P, N], I32)
-        w3s = tile("w3s", [P, N], U8)
 
         deal(nc, w2w[:], w2w_in[:])
         nc.vector.tensor_copy(out=qs[:], in_=xs[:].indirect(offs_sb[:]))
@@ -117,16 +121,22 @@ def tile_picked_maskdec_relu_po_kernel(
         mw = stage.tile([P, S], U32, name="mw", align_bytes=64, offset=4 * HALF)
         nc.vector.tensor_copy(out=mw[:], in_=xw[:].bitcast(U32).indirect(mix_sb[:]))
 
-        w1_bf = tile("w1_bf", [P, H * PACK], BF16)
-        nc.vector.tensor_copy(
-            out=w1_bf[:].rearrange("p (t m j) -> p m j t", t=PACK, j=PACK),
-            in_=w1_raw[:].rearrange("p j (m t) -> p m j t", t=PACK),
-        )
-        deal(nc, w3w[:], w3w_in[:])
+        w1_bf = stage.tile([P, H * PACK], BF16, name="w1_bf", align_bytes=64, offset=ROUNDED_AT)
+        for u in range(2):
+            pair = slice(2 * u, 2 * u + 2)
+            nc.vector.tensor_copy(
+                out=w1_bf[:].rearrange("p (t m j) -> p m j t", t=PACK, j=PACK)[:, :, :, pair],
+                in_=w1_raw[:].rearrange("p j (m t) -> p m j t", t=PACK)[:, :, :, pair],
+            )
         w1w = tile("w1w", [P, H], U32)
         w1s = tile("w1s", [P, H], U8)
-        nc.vector.quantize_mx(out=w1w[:].bitcast(FP8X4), scales=w1s[:], in_=w1_bf[:])
-        deal_bytes(nc, w3s[:], w3s_in[:])
+        for u in range(2):
+            cols = slice(u * H // 2, (u + 1) * H // 2)
+            nc.vector.quantize_mx(out=w1w[:, cols].bitcast(FP8X4), scales=w1s[:, cols], in_=w1_bf[:, PACK * cols.start : PACK * cols.stop])
+        w3w = stage.tile([P, N], I32, name="w3w", align_bytes=64, offset=ROUNDED_AT)
+        w3s = stage.tile([P, N], U8, name="w3s", align_bytes=64, offset=ROUNDED_AT + 4 * N)
+        deal_on_gpsimd(nc, w3w[:], w3w_in[:])
+        deal_on_gpsimd(nc, w3s[:], w3s_in[:])
 
         picked = [tile(f"mask{g}", [P, PACK, LOOKUP], F32) for g in range(S // LOOKUP)]
 
@@ -148,13 +158,17 @@ def tile_picked_maskdec_relu_po_kernel(
         out_rows = out_0.rearrange("(p t) n -> p t n", t=PACK)
         out_words = words_of(out_1)
         e_ps = []
-        for c in range(chunks):
+
+        def encode(c):
             cols = slice(c * CHUNK, (c + 1) * CHUNK)
-            bank = psum.tile([P, PACK, CHUNK], F32, name=f"e_ps{c}", tag=f"bank{c}")
+            bank = psum.tile([P, PACK, CHUNK], F32, name=f"e_ps{c}", tag=f"bank{c % E_BANKS}")
             for t in range(PACK):
                 rows = slice(t * P, (t + 1) * P)
                 mx(nc, bank[:, t, :], w1w[:, rows], w1s[:, rows], mw[:, cols], ms[:, cols])
             e_ps.append(bank)
+
+        for c in range(E_BANKS):
+            encode(c)
 
         y = [tile(f"y{chunk}", [P, PACK, CHUNK], F32) for chunk in range(chunks)]
         z_bf, y_ps, y_sb, y_bf = {}, {}, {}, {}
@@ -207,6 +221,7 @@ def tile_picked_maskdec_relu_po_kernel(
             queue.dma_start(out=out_words[:, cols], in_=yw[:, cols])
 
         masked(0)
+        encode(3)
         masked(1)
         decode(0)
         look_up_on_vector(1)

@@ -23,6 +23,7 @@ PIECES = ((0, 128), (128, 128), (256, 128), (384, 64), (448, 64))
 ON_VECTOR = 1
 ON_SCALAR = ((0, 256), (256, 128), (384, 128))
 HALF = S // 2
+SHARED = 128
 E_BANKS = 3
 ROUNDED_AT = 4096
 
@@ -38,10 +39,6 @@ def words_of(dram):
 
 def deal(nc, dealt, plain):
     nc.vector.tensor_copy(out=dealt.rearrange("p (t m) -> p m t", t=PACK), in_=plain.rearrange("p (m t) -> p m t", t=PACK))
-
-
-def deal_bytes(nc, dealt, plain):
-    nc.vector.tensor_copy(out=dealt.rearrange("p (t m) -> p t m", t=PACK), in_=plain.rearrange("p (m t) -> p t m", t=PACK))
 
 
 def deal_on_gpsimd(nc, dealt, plain):
@@ -72,7 +69,7 @@ def tile_picked_maskdec_relu_po_kernel(
         xs = tile("xs", [P, T], U8)
         w1_raw = tile("w1_raw", [P, PACK, H], F32)
         w2w_in = tile("w2w_in", [P, H], I32)
-        w2s_in = stage.tile([P, H], U8, name="w2s_in", align_bytes=64, offset=4 * HALF - H // 2)
+        w2s_in = tile("w2s_in", [P, H], U8)
         w3w_in = tile("w3w_in", [P, N], I32)
         w3s_in = tile("w3s_in", [P, N], U8)
 
@@ -99,26 +96,27 @@ def tile_picked_maskdec_relu_po_kernel(
         deal(nc, w2w[:], w2w_in[:])
         nc.vector.tensor_copy(out=qs[:], in_=xs[:].indirect(offs_sb[:]))
         nc.vector.tensor_copy(out=ms[:], in_=xs[:].indirect(mix_sb[:]))
-        deal_bytes(nc, w2s[:], w2s_in[:])
+        for u in range(2):
+            pair = slice(2 * u, 2 * u + 2)
+            nc.gpsimd.tensor_copy(
+                out=w2s[:].rearrange("p (t m) -> p t m", t=PACK)[:, pair, :], in_=w2s_in[:].rearrange("p (m t) -> p t m", t=PACK)[:, pair, :]
+            )
 
         s_sb = [tile(f"s_sb{t}", [P, S], F32) for t in range(PACK)]
         for h in range(2):
             half = slice(h * HALF, (h + 1) * HALF)
-            if h == 0:
-                qw = tile("qw0", [P, HALF], U32)
-            else:
-                qw = stage.tile([P, HALF], U32, name="qw1", align_bytes=64, offset=0)
+            qw = tile(f"qw{h}", [P, HALF], U32)
             nc.vector.tensor_copy(out=qw[:], in_=xw[:].bitcast(U32).indirect(offs_sb[:, h * HALF // 16 : (h + 1) * HALF // 16]))
             for t in range(PACK):
                 rows = slice(t * P, (t + 1) * P)
                 s_ps = psum.tile([P, HALF], F32, name=f"s_ps{h}{t}", tag=f"bank{h * PACK + t}")
                 mx(nc, s_ps[:], w2w[:, rows], w2s[:, rows], qw[:], qs[:, half])
-                if t < ON_VECTOR:
+                if t < 2:
                     nc.scalar.activation(out=s_sb[t][:, half], in_=s_ps[:], func=ACT.Sigmoid)
                 else:
                     nc.scalar.copy(out=s_sb[t][:, half], in_=s_ps[:])
 
-        mw = stage.tile([P, S], U32, name="mw", align_bytes=64, offset=4 * HALF)
+        mw = tile("mw", [P, S], U32)
         nc.vector.tensor_copy(out=mw[:], in_=xw[:].bitcast(U32).indirect(mix_sb[:]))
 
         w1_bf = stage.tile([P, H * PACK], BF16, name="w1_bf", align_bytes=64, offset=ROUNDED_AT)
@@ -147,11 +145,14 @@ def tile_picked_maskdec_relu_po_kernel(
             for t in range(ON_VECTOR):
                 nc.vector.tensor_copy(out=picked[g][:, t, :], in_=window(t, g * LOOKUP, LOOKUP))
 
+        if SHARED < LOOKUP:
+            nc.scalar.activation(out=picked[0][:, 1, SHARED:], in_=window(1, SHARED, LOOKUP - SHARED), func=ACT.Copy)
         for first, width in ON_SCALAR:
-            for t in range(ON_VECTOR, PACK):
+            for t in range(1 if first else 2, PACK):
                 out = picked[first // LOOKUP][:, t, first % LOOKUP : first % LOOKUP + width]
-                nc.scalar.activation(out=out, in_=window(t, first, width), func=ACT.Sigmoid)
+                nc.scalar.activation(out=out, in_=window(t, first, width), func=ACT.Copy if t < 2 else ACT.Sigmoid)
         look_up_on_vector(0)
+        nc.vector.tensor_copy(out=picked[0][:, 1, :SHARED], in_=window(1, 0, SHARED))
 
         yw = tile("yw", [P, S], I32)
         ys = tile("ys", [P, S], U8)

@@ -23,7 +23,6 @@ PIECES = ((0, 128), (128, 128), (256, 128), (384, 64), (448, 64))
 ON_VECTOR = 1
 ON_SCALAR = ((0, 256), (256, 128), (384, 128))
 HALF = S // 2
-SHARED = 128
 E_BANKS = 3
 ROUNDED_AT = 4096
 
@@ -111,7 +110,7 @@ def tile_picked_maskdec_relu_po_kernel(
                 rows = slice(t * P, (t + 1) * P)
                 s_ps = psum.tile([P, HALF], F32, name=f"s_ps{h}{t}", tag=f"bank{h * PACK + t}")
                 mx(nc, s_ps[:], w2w[:, rows], w2s[:, rows], qw[:], qs[:, half])
-                if t < 2:
+                if t < ON_VECTOR:
                     nc.scalar.activation(out=s_sb[t][:, half], in_=s_ps[:], func=ACT.Sigmoid)
                 else:
                     nc.scalar.copy(out=s_sb[t][:, half], in_=s_ps[:])
@@ -145,14 +144,11 @@ def tile_picked_maskdec_relu_po_kernel(
             for t in range(ON_VECTOR):
                 nc.vector.tensor_copy(out=picked[g][:, t, :], in_=window(t, g * LOOKUP, LOOKUP))
 
-        if SHARED < LOOKUP:
-            nc.scalar.activation(out=picked[0][:, 1, SHARED:], in_=window(1, SHARED, LOOKUP - SHARED), func=ACT.Copy)
         for first, width in ON_SCALAR:
-            for t in range(1 if first else 2, PACK):
+            for t in range(ON_VECTOR, PACK):
                 out = picked[first // LOOKUP][:, t, first % LOOKUP : first % LOOKUP + width]
-                nc.scalar.activation(out=out, in_=window(t, first, width), func=ACT.Copy if t < 2 else ACT.Sigmoid)
+                nc.scalar.activation(out=out, in_=window(t, first, width), func=ACT.Sigmoid)
         look_up_on_vector(0)
-        nc.vector.tensor_copy(out=picked[0][:, 1, :SHARED], in_=window(1, 0, SHARED))
 
         yw = tile("yw", [P, S], I32)
         ys = tile("ys", [P, S], U8)

@@ -36,10 +36,6 @@ def words_of(dram):
     return dram[0].rearrange("p n t -> p (n t)").bitcast(I32)
 
 
-def deal(nc, dealt, plain):
-    nc.vector.tensor_copy(out=dealt.rearrange("p (t m) -> p m t", t=PACK), in_=plain.rearrange("p (m t) -> p m t", t=PACK))
-
-
 def deal_on_gpsimd(nc, dealt, plain):
     nc.gpsimd.tensor_copy(out=dealt.rearrange("p (t m) -> p t m", t=PACK), in_=plain.rearrange("p (m t) -> p t m", t=PACK))
 
@@ -92,7 +88,7 @@ def tile_picked_maskdec_relu_po_kernel(
         w2w = tile("w2w", [P, H], I32)
         w2s = tile("w2s", [P, H], U8)
 
-        deal(nc, w2w[:], w2w_in[:])
+        deal_on_gpsimd(nc, w2w[:], w2w_in[:])
         nc.vector.tensor_copy(out=qs[:], in_=xs[:].indirect(offs_sb[:]))
         nc.vector.tensor_copy(out=ms[:], in_=xs[:].indirect(mix_sb[:]))
         for u in range(2):

@@ -75,7 +75,7 @@ def tile_picked_maskdec_relu_po_kernel(
         nc.sync.dma_start(out=offs_sb[:], in_=offs)
         nc.sync.dma_start(out=mix_sb[:], in_=mix)
         nc.sync.dma_start(out=w2w_in[:], in_=words_of(w2_words))
-        load_scale_rows([nc.sync, nc.scalar] * 2, xs, x_scales[0])
+        load_scale_rows([nc.scalar, nc.scalar, nc.sync, nc.sync], xs, x_scales[0])
         nc.sync.dma_start(out=xw[:], in_=words_of(x_words))
         load_scale_rows([nc.sync] * 4, w2s_in, w2_scales[0])
         nc.sync.dma_start(out=w1_raw[:], in_=w1.rearrange("(p j) c -> p j c", j=PACK))

@@ -68,7 +68,7 @@ def tile_picked_maskdec_relu_po_kernel(
         w3w_in = tile("w3w_in", [P, N], I32)
         w3s_in = tile("w3s_in", [P, N], U8)
 
-        nc.vector.memset(xs[:].bitcast(I32), 0)
+        nc.gpsimd.memset(xs[:].bitcast(I32), 0)
         nc.vector.memset(w2s_in[:].bitcast(I32), 0)
         nc.vector.memset(w3s_in[:].bitcast(I32), 0)
 
@@ -201,7 +201,7 @@ def tile_picked_maskdec_relu_po_kernel(
         def interleave(c):
             y_bf[c] = tile(f"y_bf{c}", [P, PIECES[c][1], PACK], BF16)
             nc.vector.tensor_copy(
-                out=y_bf[c][:].rearrange("p (b i) t -> p b t i", i=4), in_=y_sb[c].rearrange("p t (b i) -> p b t i", i=4)
+                out=y_bf[c][:].rearrange("p (b i) t -> p b t i", i=2), in_=y_sb[c].rearrange("p t (b i) -> p b t i", i=2)
             )
 
         def planes(c):

@@ -21,7 +21,7 @@ CHUNK = 128
 LOOKUP = 256
 PIECES = ((0, 128), (128, 128), (256, 128), (384, 64), (448, 64))
 ON_VECTOR = 1
-ON_SCALAR = ((0, 256), (256, 128), (384, 128))
+ON_SCALAR = ((0, 128), (128, 128), (256, 128), (384, 128))
 HALF = S // 2
 E_BANKS = 3
 ROUNDED_AT = 4096

@@ -24,6 +24,7 @@ ON_VECTOR = 1
 ON_SCALAR = ((0, 128), (128, 128), (256, 128), (384, 128))
 HALF = S // 2
 E_BANKS = 3
+Y_BANKS = ((4,), (5,), (6, 1), (7,), (0, 2))
 ROUNDED_AT = 4096
 
 
@@ -185,24 +186,33 @@ def tile_picked_maskdec_relu_po_kernel(
             zw = tile(f"zw{c}", [P, width], U32)
             zs = tile(f"zs{c}", [P, width], U8)
             nc.vector.quantize_mx(out=zw[:].bitcast(FP8X4), scales=zs[:], in_=z_bf[c][:].rearrange("p n t -> p (n t)"))
-            y_ps[c] = psum.tile([P, PACK, width], F32, name=f"y_ps{c}", tag=f"bank{(PACK + c) % 8}")
+            banks = Y_BANKS[c]
+            slots = PACK // len(banks)
+            y_ps[c] = [psum.tile([P, slots, width], F32, name=f"y_ps{c}{b}", tag=f"bank{b}") for b in banks]
             for t in range(PACK):
                 rows = slice(t * P, (t + 1) * P)
-                mx(nc, y_ps[c][:, t, :], w3w[:, rows], w3s[:, rows], zw[:], zs[:])
+                mx(nc, y_ps[c][t // slots][:, t % slots, :], w3w[:, rows], w3s[:, rows], zw[:], zs[:])
 
         def leave(c):
             first, width = PIECES[c]
             chunk = first // CHUNK
             y_sb[c] = y[chunk][:, :, first % CHUNK : first % CHUNK + width]
-            nc.scalar.copy(out=y_sb[c], in_=y_ps[c][:])
+            slots = PACK // len(y_ps[c])
+            for b, bank in enumerate(y_ps[c]):
+                part = slice(b * slots, (b + 1) * slots)
+                nc.scalar.copy(out=y_sb[c][:, part, :], in_=bank[:])
             if (first + width) % CHUNK == 0:
                 nc.sync.dma_start(out=out_rows[:, :, chunk * CHUNK : (chunk + 1) * CHUNK], in_=y[chunk][:])
 
         def interleave(c):
             y_bf[c] = tile(f"y_bf{c}", [P, PIECES[c][1], PACK], BF16)
-            nc.vector.tensor_copy(
-                out=y_bf[c][:].rearrange("p (b i) t -> p b t i", i=2), in_=y_sb[c].rearrange("p t (b i) -> p b t i", i=2)
-            )
+            if c == len(PIECES) - 1:
+                for b, bank in enumerate(y_ps[c]):
+                    nc.scalar.copy(out=y_bf[c][:, :, 2 * b : 2 * b + 2], in_=bank[:].rearrange("p t n -> p n t"))
+            else:
+                nc.vector.tensor_copy(
+                    out=y_bf[c][:].rearrange("p (b i) t -> p b t i", i=2), in_=y_sb[c].rearrange("p t (b i) -> p b t i", i=2)
+                )
 
         def planes(c):
             first, width = PIECES[c]

@@ -24,7 +24,7 @@ ON_VECTOR = 1
 ON_SCALAR = ((0, 128), (128, 128), (256, 128), (384, 128))
 HALF = S // 2
 E_BANKS = 3
-Y_BANKS = ((4,), (5,), (6, 1), (7,), (0, 2))
+Y_BANKS = ((4, 3), (5, 1), (6, 2), (7,), (0, 4))
 ROUNDED_AT = 4096
 
 
@@ -115,20 +115,20 @@ def tile_picked_maskdec_relu_po_kernel(
         mw = tile("mw", [P, S], U32)
         nc.vector.tensor_copy(out=mw[:], in_=xw[:].bitcast(U32).indirect(mix_sb[:]))
 
-        w1_bf = stage.tile([P, H * PACK], BF16, name="w1_bf", align_bytes=64, offset=ROUNDED_AT)
+        w1_bf = [stage.tile([P, 2, P, PACK], BF16, name="w1_bf0", align_bytes=64, offset=ROUNDED_AT), tile("w1_bf1", [P, 2, P, PACK], BF16)]
         for u in range(2):
             pair = slice(2 * u, 2 * u + 2)
             nc.vector.tensor_copy(
-                out=w1_bf[:].rearrange("p (t m j) -> p m j t", t=PACK, j=PACK)[:, :, :, pair],
+                out=w1_bf[u][:].rearrange("p t m j -> p m j t"),
                 in_=w1_raw[:].rearrange("p j (m t) -> p m j t", t=PACK)[:, :, :, pair],
             )
         w1w = tile("w1w", [P, H], U32)
         w1s = tile("w1s", [P, H], U8)
         for u in range(2):
             cols = slice(u * H // 2, (u + 1) * H // 2)
-            nc.vector.quantize_mx(out=w1w[:, cols].bitcast(FP8X4), scales=w1s[:, cols], in_=w1_bf[:, PACK * cols.start : PACK * cols.stop])
-        w3w = stage.tile([P, N], I32, name="w3w", align_bytes=64, offset=ROUNDED_AT)
-        w3s = stage.tile([P, N], U8, name="w3s", align_bytes=64, offset=ROUNDED_AT + 4 * N)
+            nc.vector.quantize_mx(out=w1w[:, cols].bitcast(FP8X4), scales=w1s[:, cols], in_=w1_bf[u][:].rearrange("p t m j -> p (t m j)"))
+        w3w = stage.tile([P, N], I32, name="w3w", align_bytes=64, offset=ROUNDED_AT + N)
+        w3s = stage.tile([P, N], U8, name="w3s", align_bytes=64, offset=ROUNDED_AT)
         deal_on_gpsimd(nc, w3w[:], w3w_in[:])
         deal_on_gpsimd(nc, w3s[:], w3s_in[:])
 

@@ -244,14 +244,14 @@ def tile_picked_maskdec_relu_po_kernel(
         interleave(1)
         planes(0)
         planes(1)
-        store_words(nc.sync, 0, 1)
         interleave(2)
         interleave(3)
         planes(2)
+        store_words(nc.sync, 0, 2)
         interleave(4)
         planes(3)
         planes(4)
-        store_words(nc.scalar, 2, 4)
+        store_words(nc.scalar, 3, 4)
 
         for r, queue in enumerate((nc.sync, nc.sync, nc.scalar, nc.sync)):
             queue.dma_start(out=out_2[0][r:16:4, :].bitcast(I32), in_=ys[r:P:32, :].bitcast(I32))

from contextlib import ExitStack

import concourse.mybir as mybir

K, T, S, H, N = 512, 2048, 512, 512, 512
FLOPS = 2 * K * H * S + 2 * K * H * S + 2 * H * N * S

F32 = mybir.dt.float32
BF16 = mybir.dt.bfloat16
I32 = mybir.dt.int32
U32 = mybir.dt.uint32
U16 = mybir.dt.uint16
U8 = mybir.dt.uint8
FP8X4 = mybir.dt.float8_e4m3fn_x4
ALU = mybir.AluOpType
ACT = mybir.ActivationFunctionType

P = 128
PACK = 4
CHUNK = 128
LOOKUP = 256
PIECES = ((0, 128), (128, 128), (256, 128), (384, 64), (448, 64))
ON_VECTOR = 1
ON_SCALAR = ((0, 128), (128, 128), (256, 128), (384, 128))
HALF = S // 2
E_BANKS = 3
Y_BANKS = ((4, 3), (5, 1), (6, 2), (7,), (0, 4))
ROUNDED_AT = 4096


def load_scale_rows(queues, plane, rows):
    for r, queue in enumerate(queues):
        queue.dma_start(out=plane[r:P:32, :].bitcast(I32), in_=rows[r:16:4, :].bitcast(I32))


def words_of(dram):
    return dram[0].rearrange("p n t -> p (n t)").bitcast(I32)


def deal_on_gpsimd(nc, dealt, plain):
    nc.gpsimd.tensor_copy(out=dealt.rearrange("p (t m) -> p t m", t=PACK), in_=plain.rearrange("p (m t) -> p t m", t=PACK))


def mx(nc, out, w_words, w_scales, a_words, a_scales):
    nc.tensor.matmul_mx(out=out, lhsT=w_words.bitcast(FP8X4), lhsT_scale=w_scales, rhs=a_words.bitcast(FP8X4), rhs_scale=a_scales, start=True, stop=True)


def tile_picked_maskdec_relu_po_kernel(
    tc, x_words, x_scales, w1, w2_words, w2_scales, w3_words, w3_scales, offs, mix, al, out_0, out_1, out_2
):
    nc = tc.nc
    chunks = S // CHUNK
    with ExitStack() as ctx:
        keep = ctx.enter_context(tc.tile_pool(name="keep", bufs=1))
        stage = ctx.enter_context(tc.tile_pool(name="stage", bufs=1))
        psum = ctx.enter_context(tc.psum_pool(name="psum", bufs=1))

        def tile(name, shape, dtype, tag=None):
            return keep.tile(shape, dtype, name=name, tag=tag or name, align_bytes=64)

        offs_sb = tile("offs_sb", [P, S // 16], U16)
        mix_sb = tile("mix_sb", [P, S // 16], U16)
        al_sb = tile("al_sb", [P, S // 16], U16)
        xw = tile("xw", [P, T], I32)
        xs = tile("xs", [P, T], U8)
        w1_raw = tile("w1_raw", [P, PACK, H], F32)
        w2w_in = tile("w2w_in", [P, H], I32)
        w2s_in = tile("w2s_in", [P, H], U8)
        w3w_in = tile("w3w_in", [P, N], I32)
        w3s_in = tile("w3s_in", [P, N], U8)

        nc.gpsimd.memset(xs[:].bitcast(I32), 0)
        nc.vector.memset(w2s_in[:].bitcast(I32), 0)
        nc.vector.memset(w3s_in[:].bitcast(I32), 0)

        nc.sync.dma_start(out=offs_sb[:], in_=offs)
        nc.sync.dma_start(out=mix_sb[:], in_=mix)
        nc.sync.dma_start(out=w2w_in[:], in_=words_of(w2_words))
        load_scale_rows([nc.scalar, nc.scalar, nc.sync, nc.sync], xs, x_scales[0])
        nc.sync.dma_start(out=xw[:], in_=words_of(x_words))
        load_scale_rows([nc.sync] * 4, w2s_in, w2_scales[0])
        nc.sync.dma_start(out=w1_raw[:], in_=w1.rearrange("(p j) c -> p j c", j=PACK))
        nc.sync.dma_start(out=al_sb[:], in_=al)
        nc.sync.dma_start(out=w3w_in[:], in_=words_of(w3_words))
        load_scale_rows([nc.sync] * 4, w3s_in, w3_scales[0])

        qs = tile("qs", [P, S], U8)
        ms = tile("ms", [P, S], U8)
        w2w = tile("w2w", [P, H], I32)
        w2s = tile("w2s", [P, H], U8)

        deal_on_gpsimd(nc, w2w[:], w2w_in[:])
        nc.vector.tensor_copy(out=qs[:], in_=xs[:].indirect(offs_sb[:]))
        nc.vector.tensor_copy(out=ms[:], in_=xs[:].indirect(mix_sb[:]))
        for u in range(2):
            pair = slice(2 * u, 2 * u + 2)
            nc.gpsimd.tensor_copy(
                out=w2s[:].rearrange("p (t m) -> p t m", t=PACK)[:, pair, :], in_=w2s_in[:].rearrange("p (m t) -> p t m", t=PACK)[:, pair, :]
            )

        s_sb = [tile(f"s_sb{t}", [P, S], F32) for t in range(PACK)]
        for h in range(2):
            half = slice(h * HALF, (h + 1) * HALF)
            qw = tile(f"qw{h}", [P, HALF], U32)
            nc.vector.tensor_copy(out=qw[:], in_=xw[:].bitcast(U32).indirect(offs_sb[:, h * HALF // 16 : (h + 1) * HALF // 16]))
            for t in range(PACK):
                rows = slice(t * P, (t + 1) * P)
                s_ps = psum.tile([P, HALF], F32, name=f"s_ps{h}{t}", tag=f"bank{h * PACK + t}")
                mx(nc, s_ps[:], w2w[:, rows], w2s[:, rows], qw[:], qs[:, half])
                if t < ON_VECTOR:
                    nc.scalar.activation(out=s_sb[t][:, half], in_=s_ps[:], func=ACT.Sigmoid)
                else:
                    nc.scalar.copy(out=s_sb[t][:, half], in_=s_ps[:])

        mw = tile("mw", [P, S], U32)
        nc.vector.tensor_copy(out=mw[:], in_=xw[:].bitcast(U32).indirect(mix_sb[:]))

        w1_bf = [stage.tile([P, 2, P, PACK], BF16, name="w1_bf0", align_bytes=64, offset=ROUNDED_AT), tile("w1_bf1", [P, 2, P, PACK], BF16)]
        for u in range(2):
            pair = slice(2 * u, 2 * u + 2)
            nc.vector.tensor_copy(
                out=w1_bf[u][:].rearrange("p t m j -> p m j t"),
                in_=w1_raw[:].rearrange("p j (m t) -> p m j t", t=PACK)[:, :, :, pair],
            )
        w1w = tile("w1w", [P, H], U32)
        w1s = tile("w1s", [P, H], U8)
        for u in range(2):
            cols = slice(u * H // 2, (u + 1) * H // 2)
            nc.vector.quantize_mx(out=w1w[:, cols].bitcast(FP8X4), scales=w1s[:, cols], in_=w1_bf[u][:].rearrange("p t m j -> p (t m j)"))
        w3w = stage.tile([P, N], I32, name="w3w", align_bytes=64, offset=ROUNDED_AT + N)
        w3s = stage.tile([P, N], U8, name="w3s", align_bytes=64, offset=ROUNDED_AT)
        deal_on_gpsimd(nc, w3w[:], w3w_in[:])
        deal_on_gpsimd(nc, w3s[:], w3s_in[:])

        picked = [tile(f"mask{g}", [P, PACK, LOOKUP], F32) for g in range(S // LOOKUP)]

        def window(t, first, width):
            return s_sb[t][:].indirect(al_sb[:, first // 16 : (first + width) // 16])

        def look_up_on_vector(g):
            for t in range(ON_VECTOR):
                nc.vector.tensor_copy(out=picked[g][:, t, :], in_=window(t, g * LOOKUP, LOOKUP))

        for first, width in ON_SCALAR:
            for t in range(ON_VECTOR, PACK):
                out = picked[first // LOOKUP][:, t, first % LOOKUP : first % LOOKUP + width]
                nc.scalar.activation(out=out, in_=window(t, first, width), func=ACT.Sigmoid)
        look_up_on_vector(0)

        yw = tile("yw", [P, S], I32)
        ys = tile("ys", [P, S], U8)
        out_rows = out_0.rearrange("(p t) n -> p t n", t=PACK)
        out_words = words_of(out_1)
        e_ps = []

        def encode(c):
            cols = slice(c * CHUNK, (c + 1) * CHUNK)
            bank = psum.tile([P, PACK, CHUNK], F32, name=f"e_ps{c}", tag=f"bank{c % E_BANKS}")
            for t in range(PACK):
                rows = slice(t * P, (t + 1) * P)
                mx(nc, bank[:, t, :], w1w[:, rows], w1s[:, rows], mw[:, cols], ms[:, cols])
            e_ps.append(bank)

        for c in range(E_BANKS):
            encode(c)

        y = [tile(f"y{chunk}", [P, PACK, CHUNK], F32) for chunk in range(chunks)]
        z_bf, y_ps, y_sb, y_bf = {}, {}, {}, {}

        def masked(c):
            first, width = PIECES[c]
            in_bank = slice(first % CHUNK, first % CHUNK + width)
            in_group = slice(first % LOOKUP, first % LOOKUP + width)
            z_bf[c] = tile(f"z_bf{c}", [P, width, PACK], BF16)
            nc.vector.scalar_tensor_tensor(
                out=z_bf[c][:],
                in0=e_ps[first // CHUNK][:, :, in_bank].rearrange("p t n -> p n t"),
                scalar=0.0,
                in1=picked[first // LOOKUP][:, :, in_group].rearrange("p t n -> p n t"),
                op0=ALU.max,
                op1=ALU.mult,
            )

        def decode(c):
            width = PIECES[c][1]
            zw = tile(f"zw{c}", [P, width], U32)
            zs = tile(f"zs{c}", [P, width], U8)
            nc.vector.quantize_mx(out=zw[:].bitcast(FP8X4), scales=zs[:], in_=z_bf[c][:].rearrange("p n t -> p (n t)"))
            banks = Y_BANKS[c]
            slots = PACK // len(banks)
            y_ps[c] = [psum.tile([P, slots, width], F32, name=f"y_ps{c}{b}", tag=f"bank{b}") for b in banks]
            for t in range(PACK):
                rows = slice(t * P, (t + 1) * P)
                mx(nc, y_ps[c][t // slots][:, t % slots, :], w3w[:, rows], w3s[:, rows], zw[:], zs[:])

        def leave(c):
            first, width = PIECES[c]
            chunk = first // CHUNK
            y_sb[c] = y[chunk][:, :, first % CHUNK : first % CHUNK + width]
            slots = PACK // len(y_ps[c])
            for b, bank in enumerate(y_ps[c]):
                part = slice(b * slots, (b + 1) * slots)
                nc.scalar.copy(out=y_sb[c][:, part, :], in_=bank[:])
            if (first + width) % CHUNK == 0:
                nc.sync.dma_start(out=out_rows[:, :, chunk * CHUNK : (chunk + 1) * CHUNK], in_=y[chunk][:])

        def interleave(c):
            y_bf[c] = tile(f"y_bf{c}", [P, PIECES[c][1], PACK], BF16)
            if c == len(PIECES) - 1:
                for b, bank in enumerate(y_ps[c]):
                    nc.scalar.copy(out=y_bf[c][:, :, 2 * b : 2 * b + 2], in_=bank[:].rearrange("p t n -> p n t"))
            else:
                nc.vector.tensor_copy(
                    out=y_bf[c][:].rearrange("p (b i) t -> p b t i", i=2), in_=y_sb[c].rearrange("p t (b i) -> p b t i", i=2)
                )

        def planes(c):
            first, width = PIECES[c]
            cols = slice(first, first + width)
            nc.vector.quantize_mx(out=yw[:, cols].bitcast(FP8X4), scales=ys[:, cols], in_=y_bf[c][:].rearrange("p n t -> p (n t)"))

        def store_words(queue, first, last):
            cols = slice(PIECES[first][0], sum(PIECES[last]))
            queue.dma_start(out=out_words[:, cols], in_=yw[:, cols])

        masked(0)
        encode(3)
        masked(1)
        decode(0)
        look_up_on_vector(1)
        decode(1)
        masked(2)
        leave(0)
        leave(1)
        masked(3)
        decode(2)
        masked(4)
        decode(3)
        interleave(0)
        decode(4)
        leave(2)
        leave(3)
        leave(4)
        interleave(1)
        planes(0)
        planes(1)
        interleave(2)
        interleave(3)
        planes(2)
        store_words(nc.sync, 0, 2)
        interleave(4)
        planes(3)
        planes(4)
        store_words(nc.scalar, 3, 4)

        for r, queue in enumerate((nc.sync, nc.sync, nc.scalar, nc.sync)):
            queue.dma_start(out=out_2[0][r:16:4, :].bitcast(I32), in_=ys[r:P:32, :].bitcast(I32))
